import numpy as np
import ml_dtypes


def mxq(x, axis, fmt="e4m3"):
    dtype, down = {"e4m3": (ml_dtypes.float8_e4m3fn, 7), "e5m2": (ml_dtypes.float8_e5m2, 14)}[fmt]
    v = np.moveaxis(np.asarray(x, np.float32).astype(ml_dtypes.bfloat16).astype(np.float64), axis, -1)
    blocks = v.reshape(v.shape[:-1] + (-1, 32))
    amax = np.abs(blocks).max(-1, keepdims=True)
    byte = np.maximum(np.where(amax > 0, np.frexp(amax)[1] - 1 + 127, 0) - down, 1)
    scale = np.exp2(byte - 127.0)
    codes = (blocks / scale).astype(np.float32).astype(dtype).astype(np.float64)
    return np.moveaxis((codes * scale).reshape(v.shape), -1, axis)


WIDE = False


def mx_kscale(k):
    if not WIDE:
        return np.ones(k)
    levels = np.array([10, -10, 5, -5, 0])
    if k % 512:
        return np.exp2(np.random.permutation(np.resize(levels, k // 32))).repeat(32)
    a = np.empty((k // 512, 16))
    for p in range(k // 512):
        a[p, :8] = np.random.permutation(np.resize(levels, 8))
        for g in range(8):
            far = levels[np.abs(levels - a[p, g]) >= 10]
            a[p, g + 8] = far[np.random.randint(len(far))]
    return np.exp2(a.ravel()).repeat(32)


def f64(x):
    return np.asarray(x).astype(np.float64)


def striped(idx):
    return np.tile(idx.reshape(-1, 16).T, (8, 1)).astype(np.uint16)


def unstriped(offs):
    return offs[:16].T.reshape(-1).astype(np.int64)


def pack_weight(w):
    k, n = w.shape
    w = f64(np.asarray(w, np.float32).astype(ml_dtypes.bfloat16)).reshape(k // 32, 32, n)
    amax = np.abs(w).max(1)
    byte = np.clip(np.where(amax > 0, np.frexp(amax)[1] - 1 + 127 - 7, 1), 1, 254)
    scaled = (w * np.exp2(127.0 - byte)[:, None, :]).reshape(k, n).astype(np.float32)
    words = np.ascontiguousarray(scaled.reshape(k // 512, 128, 4, n).transpose(0, 1, 3, 2)).astype(ml_dtypes.float8_e4m3fn).view(np.uint8)
    return words, np.ascontiguousarray(byte.astype(np.uint8).reshape(k // 512, 16, n))


def unpack_weight(words, scales):
    g, p, n, _ = words.shape
    vals = np.ascontiguousarray(words).view(ml_dtypes.float8_e4m3fn).astype(np.float64) * np.repeat(np.exp2(scales.astype(np.float64) - 127.0), 8, axis=1)[..., None]
    return vals.transpose(0, 1, 3, 2).reshape(g * 512, n)


K, T, S, D, N = 1024, 2048, 512, 4, 256
P = 2 ** 7


def setup_inputs():
    n = np.random.standard_normal
    s = mx_kscale(K)[:, None]
    packed_xT = pack_weight(n((K, T)) * s)
    return {
        "x_words": packed_xT[0],
        "x_scales": packed_xT[1],
        "w1": (n((K, N)) / np.sqrt(K) / s).astype(np.float32),
        "w2": (n((K, N)) / np.sqrt(K) / s).astype(np.float32),
        "te": (np.tile(np.random.uniform(0.1, 1.5, S), (P, 1))).astype(np.float32),
        "sig": (np.random.uniform(0.1, 1.5, (N, S))).astype(np.float32),
        "offs": striped(np.random.permutation(T)[:S]),
    }


def reference(x_words, x_scales, w1, w2, te, sig, offs):
    xq = unpack_weight(x_words, x_scales)[:, unstriped(offs)]
    yr = mxq(f64(w2), 0, "e4m3").T @ xq
    sr = np.log(np.exp(yr) + 1.0)
    rel = sr.reshape(len(sr), -1, D).mean(axis=2)
    dec = np.exp(-1.0 * (np.repeat(rel, D, axis=1) * f64(te)[:1]))
    haa0 = (dec) ** 2
    haa = haa0.reshape(len(haa0), -1, D).sum(axis=2)
    ya = mxq(f64(w1), 0, "e4m3").T @ xq
    sa = np.log(np.exp(ya) + 1.0)
    amp = sa.reshape(len(sa), -1, D).mean(axis=2) + 0.3
    jr = (-1.0 * (f64(te)[:1] * dec)) * np.repeat(amp, D, axis=1)
    res = f64(sig) - (np.repeat(amp, D, axis=1) * dec)
    gr0 = jr * res
    gr = gr0.reshape(len(gr0), -1, D).sum(axis=2)
    har0 = dec * jr
    har = har0.reshape(len(har0), -1, D).sum(axis=2)
    ga0 = dec * res
    ga = ga0.reshape(len(ga0), -1, D).sum(axis=2)
    hrr0 = (jr) ** 2
    hrr = hrr0.reshape(len(hrr0), -1, D).sum(axis=2)
    det = (haa + 0.1) * (hrr + 0.3) - ((har) ** 2)
    return rel + ((haa + 0.1) * gr - (har * ga)) / det

@@ -1,0 +1,246 @@
+from contextlib import ExitStack
+
+import concourse.mybir as mybir
+from concourse.masks import make_identity
+
+K, T, S, D, N = 1024, 2048, 512, 4, 256
+V = S // D
+P = 128
+PACK = 4
+K_PASS = P * PACK
+PASSES = K // K_PASS
+BLOCKS = N // P
+FLOPS = 2 * 2 * K * S * N
+BYTES = K * T + K * T // 32 + 2 * K * N * 4 + S * 4 + N * S * 4 + P * (S // 16) * 2 + N * V * 4
+
+F32 = mybir.dt.float32
+BF16 = mybir.dt.bfloat16
+I32 = mybir.dt.int32
+U32 = mybir.dt.uint32
+U16 = mybir.dt.uint16
+U8 = mybir.dt.uint8
+FP8X4 = mybir.dt.float8_e4m3fn_x4
+ALU = mybir.AluOpType
+ACT = mybir.ActivationFunctionType
+
+
+def tile_picked_rate_p_kernel(tc, x_words, x_scales, w1, w2, te, sig, offs, out):
+    nc = tc.nc
+    with ExitStack() as ctx:
+        keep = ctx.enter_context(tc.tile_pool(name="keep", bufs=1))
+        psum = ctx.enter_context(tc.psum_pool(name="psum", bufs=1))
+
+        def sb(name, shape, dtype=F32, tag=None):
+            return keep.tile(shape, dtype, name=name, tag=tag or name, align_bytes=64)
+
+        def bank(tag, shape):
+            return psum.tile(shape, F32, name=tag, tag=tag)
+
+        offsets = keep.tile([P, S // 16], U16, name="offsets")
+        nc.sync.dma_start(offsets[:], offs)
+        scale_rows = sb("scale_rows", [P, T], U8)
+        nc.gpsimd.memset(scale_rows[:].bitcast(I32), 0)
+        for quad in range(4):
+            nc.gpsimd.dma_start(
+                out=scale_rows[32 * quad : 32 * quad + 4 * PASSES, :].bitcast(I32),
+                in_=x_scales[:, 4 * quad : 4 * quad + 4, :].bitcast(I32),
+            )
+        te_col = sb("te_col", [P, D])
+        nc.scalar.dma_start(out=te_col[:], in_=te[0:1, :].rearrange("o (v d) -> v (o d)", d=D))
+
+        def load_w(name, w, g):
+            raw = sb("%s_raw%d" % (name, g), [P, PACK, N])
+            nc.sync.dma_start(out=raw[:], in_=w[g * K_PASS : (g + 1) * K_PASS, :].rearrange("(p j) m -> p j m", j=PACK))
+            return raw
+
+        table = []
+        for g in range(PASSES):
+            words = sb("table%d" % g, [P, T], U32)
+            nc.sync.dma_start(out=words[:].bitcast(I32), in_=x_words[g].rearrange("p n t -> p (n t)").bitcast(I32))
+            table.append(words)
+        w2_raw = [load_w("w2", w2, g) for g in range(PASSES)]
+        w1_raw = [load_w("w1", w1, g) for g in range(PASSES)]
+        sig_sb = sb("sig_sb", [P, BLOCKS, S])
+        nc.sync.dma_start(out=sig_sb[:], in_=sig.rearrange("(b p) j -> p b j", p=P))
+
+        ident = sb("ident", [P, P])
+        make_identity(nc, ident[:])
+
+        te_q = sb("te_q", [P, D])
+        te_h = sb("te_h", [P, D])
+        nc.scalar.activation(te_q[:], te_col[:], ACT.Copy, scale=-1.0 / D)
+        nc.scalar.activation(te_h[:], te_col[:], ACT.Copy, scale=-2.0 / D)
+
+        def quantise(name, raw, b, grouped, on_scalar):
+            dst = grouped.rearrange("p (c i t) -> p c t i", i=4, t=PACK)
+            src = raw[:, :, b * P : (b + 1) * P].rearrange("p t (c i) -> p c t i", i=4)
+            if on_scalar:
+                nc.scalar.copy(dst, src)
+            else:
+                nc.vector.tensor_copy(dst, src)
+            codes = sb(name + "_codes", [P, P], U32)
+            scales = sb(name + "_scales", [P, P], U8)
+            nc.vector.quantize_mx(out=codes[:].bitcast(FP8X4), scales=scales[:], in_=grouped)
+            return codes, scales
+
+        picked_scales = sb("picked_scales", [P, S], U8)
+        picked = [sb("picked%d" % g, [P, S], U32) for g in range(PASSES)]
+        nc.vector.tensor_copy(picked[0][:], table[0][:].indirect(offsets[:]))
+        nc.vector.tensor_copy(picked_scales[:], scale_rows[:].indirect(offsets[:]))
+        nc.vector.tensor_copy(picked[1][:], table[1][:].indirect(offsets[:]))
+
+        def product(y, w_q, g):
+            for b in range(BLOCKS):
+                codes, scales = w_q[b]
+                nc.tensor.matmul_mx(
+                    out=y[b][:],
+                    lhsT=codes[:].bitcast(FP8X4),
+                    lhsT_scale=scales[:],
+                    rhs=picked[g][:].bitcast(FP8X4),
+                    rhs_scale=picked_scales[4 * g :, :],
+                    start=(g == 0),
+                    stop=(g == PASSES - 1),
+                )
+
+        yr = [bank("y%d" % b, [P, S]) for b in range(BLOCKS)]
+        ya = [bank("y%d" % (BLOCKS + b), [P, S]) for b in range(BLOCKS)]
+        w2_bf = sb("w2_bf", [P, PASSES * BLOCKS, K_PASS], BF16, tag="scale_rows")
+        for g in range(PASSES):
+            product(yr, [quantise("w2_%d%d" % (g, b), w2_raw[g], b, w2_bf[:, g * BLOCKS + b, :], b == 1) for b in range(BLOCKS)], g)
+        w1_bf = sb("w1_bf", [P, PASSES * BLOCKS, K_PASS], BF16, tag="scale_rows")
+        for g in range(PASSES):
+            product(ya, [quantise("w1_%d%d" % (g, b), w1_raw[g], b, w1_bf[:, g * BLOCKS + b, :], False) for b in range(BLOCKS)], g)
+
+        prod = sb("prod", [P, 2 * N])
+
+        def log_argument(name, y, prod_out):
+            small = sb(name + "_small", [P, D, N])
+            for b in range(BLOCKS):
+                mag = sb("%s_mag%d" % (name, b), [P, D, V])
+                nc.scalar.activation(mag[:], y[b][:].rearrange("p (v d) -> p d v", d=D), ACT.Abs)
+                nc.scalar.activation(small[:, :, b * P : (b + 1) * P], mag[:], ACT.Exp, scale=-1.0)
+            half = sb(name + "_half", [P, 2, N])
+            nc.vector.tensor_scalar(half[:], small[:, 0:2, :], 1.0, None, ALU.add)
+            pair = sb(name + "_pair", [P, 2, N])
+            nc.vector.scalar_tensor_tensor(pair[:], small[:, 2:4, :], 1.0, half[:], ALU.add, ALU.mult)
+            nc.vector.tensor_tensor(prod_out, pair[:, 0, :], pair[:, 1, :], ALU.mult)
+
+        def relu_sum(name, y, shift):
+            relu = sb(name + "_relu", [P, N])
+            for d in range(D):
+                for b in range(BLOCKS):
+                    cols = slice(b * P, (b + 1) * P)
+                    y_d = y[b][:, d::D]
+                    if d == 0:
+                        nc.vector.tensor_scalar(relu[:, cols], y_d, 0.0, shift, ALU.max, ALU.add)
+                    else:
+                        nc.vector.scalar_tensor_tensor(relu[:, cols], y_d, 0.0, relu[:, cols], ALU.max, ALU.add)
+            return relu
+
+        log_argument("r", yr, prod[:, :N])
+        log_argument("a", ya, prod[:, N:])
+        relu_r = relu_sum("r", yr, 0.0)
+
+        sig_t = [bank("y%d" % h, [P, 2, N]) for h in range(D // 2)]
+        for d in range(D):
+            for b in range(BLOCKS):
+                nc.tensor.transpose(sig_t[d // 2][:, d % 2, b * P : (b + 1) * P], sig_sb[:, b, d::D], ident[:])
+
+        logs = sb("logs", [P, 2 * N], tag="a_mag1")
+        nc.scalar.activation(logs[:, :N], prod[:, :N], ACT.Ln)
+        nc.scalar.activation(logs[:, N:], prod[:, N:], ACT.Ln)
+        warm = sb("warm", [P, 8])
+        nc.scalar.activation(warm[:, 0:1], logs[:, N : N + 1], ACT.Exp)
+        rel4 = sb("rel4", [P, N])
+        nc.vector.tensor_tensor(rel4[:], logs[:, :N], relu_r[:], ALU.add)
+        rel4_t = bank("rel4_t", [P, N])
+        for b in range(BLOCKS):
+            cols = slice(b * P, (b + 1) * P)
+            nc.tensor.transpose(rel4_t[:, cols], rel4[:, cols], ident[:])
+        relu_a = relu_sum("a", ya, 0.3 * D)
+        amp4 = sb("amp4", [P, N])
+        nc.vector.tensor_tensor(amp4[:], logs[:, N:], relu_a[:], ALU.add)
+
+        dec = [sb("dec%d" % d, [P, N]) for d in range(D)]
+        dec_sq = [sb("dec_sq%d" % d, [P, N]) for d in range(D)]
+        tdec_sq = [sb("tdec_sq%d" % d, [P, N]) for d in range(D)]
+        dec_sig = [sb("dec_sig%d" % d, [P, N]) for d in range(D)]
+        for d in range(D):
+            nc.scalar.activation(dec_sq[d][:], rel4_t[:], ACT.Exp, scale=te_h[:, d : d + 1])
+        for d in range(D):
+            nc.scalar.activation(dec[d][:], rel4_t[:], ACT.Exp, scale=te_q[:, d : d + 1])
+        for d in range(D):
+            nc.scalar.activation(tdec_sq[d][:], dec[d][:], ACT.Square, scale=te_col[:, d : d + 1])
+
+        def weighted_sum(name, terms):
+            acc = sb(name, [P, N])
+            nc.vector.tensor_scalar(acc[:], terms[0][:], te_col[:, 0:1], None, ALU.mult)
+            for d in range(1, D):
+                nc.vector.scalar_tensor_tensor(acc[:], terms[d][:], te_col[:, d : d + 1], acc[:], ALU.mult, ALU.add)
+            return acc
+
+        halves = [slice(b * P, (b + 1) * P) for b in range(BLOCKS)]
+
+        def turned_sum(totals, terms):
+            for i, term in enumerate(terms):
+                for total, cols in zip(totals, halves):
+                    nc.tensor.matmul(total, term[:, cols], ident[:], start=(i == 0), stop=(i == len(terms) - 1), is_transpose=True)
+
+        s01 = [bank("s01_%d" % b, [P, 2, V]) for b in range(BLOCKS)]
+        s0 = [x[:, 0, :] for x in s01]
+        s1 = [x[:, 1, :] for x in s01]
+        turned_sum(s0, dec_sq)
+        turned_sum(s1, [weighted_sum("s1_v", dec_sq)])
+        har4 = sb("har4", [P, N])
+        for b, cols in enumerate(halves):
+            nc.vector.tensor_tensor(har4[:, cols], s1[b], amp4[:, cols], ALU.mult)
+        har_sq = sb("har_sq", [P, N])
+        nc.scalar.activation(har_sq[:], har4[:], ACT.Square, scale=1.0 / D)
+        nc.scalar.activation(warm[:, 1:2], har_sq[:, 0:1], ACT.Abs_reciprocal_sqrt)
+        for d in range(D):
+            nc.vector.tensor_tensor(dec_sig[d][:], sig_t[d // 2][:, d % 2, :], dec[d][:], ALU.mult)
+        t0 = [bank("y%d" % (BLOCKS + b), [P, V])[:] for b in range(BLOCKS)]
+        turned_sum(t0, dec_sig)
+        s2 = [bank("s2", [P, V])[:], bank("rel4_t", [P, V])[:]]
+        turned_sum(s2, tdec_sq)
+        t1 = [bank("y%d" % b, [P, V])[:] for b in range(BLOCKS)]
+        turned_sum(t1, [weighted_sum("t1_v", dec_sig)])
+        amp_haa4 = sb("amp_haa4", [P, N])
+        for b, cols in enumerate(halves):
+            nc.vector.scalar_tensor_tensor(amp_haa4[:, cols], s0[b], 0.1, amp4[:, cols], ALU.add, ALU.mult)
+        c1 = sb("c1", [P, N])
+        nc.vector.scalar_tensor_tensor(c1[:], amp_haa4[:], 1.0 / (D * D), amp4[:], ALU.mult, ALU.mult)
+        c0 = sb("c0", [P, N])
+        for b, cols in enumerate(halves):
+            nc.vector.scalar_tensor_tensor(c0[:, cols], s0[b], 0.3, har_sq[:, cols], ALU.mult, ALU.subtract)
+        e = sb("e", [P, N])
+        det = sb("det", [P, N])
+        root = sb("root", [P, N])
+        inv = sb("inv", [P, N])
+        for b, cols in enumerate(halves):
+            nc.vector.tensor_tensor(e[:, cols], s2[b], c1[:, cols], ALU.mult)
+        for cols in halves:
+            nc.vector.scalar_tensor_tensor(det[:, cols], c0[:, cols], 0.03, e[:, cols], ALU.add, ALU.add)
+        for cols in halves:
+            nc.scalar.activation(root[:, cols], det[:, cols], ACT.Abs_reciprocal_sqrt)
+        for cols in halves:
+            nc.scalar.activation(inv[:, cols], root[:, cols], ACT.Square, scale=0.5)
+        t0p = sb("t0p", [P, N])
+        for b, cols in enumerate(halves):
+            nc.vector.scalar_tensor_tensor(t0p[:, cols], amp4[:, cols], 0.1 / D, t0[b], ALU.mult, ALU.add)
+        n1 = sb("n1", [P, N])
+        n2 = sb("n2", [P, N])
+        num = sb("num", [P, N])
+        step = sb("step", [P, N])
+        res = sb("res", [P, N])
+        for b, cols in enumerate(halves):
+            nc.vector.tensor_tensor(n2[:, cols], t1[b], amp_haa4[:, cols], ALU.mult)
+        for cols in halves:
+            nc.vector.tensor_tensor(n1[:, cols], t0p[:, cols], har4[:, cols], ALU.mult)
+        for cols in halves:
+            nc.vector.tensor_tensor(num[:, cols], n1[:, cols], n2[:, cols], ALU.subtract)
+        for cols in halves:
+            nc.vector.tensor_tensor(step[:, cols], num[:, cols], inv[:, cols], ALU.mult)
+        for cols in halves:
+            nc.vector.scalar_tensor_tensor(res[:, cols], rel4[:, cols], 1.0 / D, step[:, cols], ALU.mult, ALU.add)
+            nc.sync.dma_start(out=out[cols, :], in_=res[:, cols])

@@ -38,38 +38,37 @@ def tile_picked_rate_p_kernel(tc, x_words, x_scales, w1, w2, te, sig, offs, out)
 
         offsets = keep.tile([P, S // 16], U16, name="offsets")
         nc.sync.dma_start(offsets[:], offs)
+        te_col = sb("te_col", [P, D])
+        nc.sync.dma_start(out=te_col[:], in_=te[0:1, :].rearrange("o (v d) -> v (o d)", d=D))
         scale_rows = sb("scale_rows", [P, T], U8)
         nc.gpsimd.memset(scale_rows[:].bitcast(I32), 0)
         for quad in range(4):
-            nc.gpsimd.dma_start(
+            nc.scalar.dma_start(
                 out=scale_rows[32 * quad : 32 * quad + 4 * PASSES, :].bitcast(I32),
                 in_=x_scales[:, 4 * quad : 4 * quad + 4, :].bitcast(I32),
             )
-        te_col = sb("te_col", [P, D])
-        nc.scalar.dma_start(out=te_col[:], in_=te[0:1, :].rearrange("o (v d) -> v (o d)", d=D))
 
-        def load_w(name, w, g):
-            raw = sb("%s_raw%d" % (name, g), [P, PACK, N])
+        def load_w(name, w, g, tag=None):
+            raw = sb("%s_raw%d" % (name, g), [P, PACK, N], tag=tag)
             nc.sync.dma_start(out=raw[:], in_=w[g * K_PASS : (g + 1) * K_PASS, :].rearrange("(p j) m -> p j m", j=PACK))
             return raw
 
+        w2_raw = [load_w("w2", w2, g, "w_raw%d" % g) for g in range(PASSES)]
         table = []
         for g in range(PASSES):
             words = sb("table%d" % g, [P, T], U32)
             nc.sync.dma_start(out=words[:].bitcast(I32), in_=x_words[g].rearrange("p n t -> p (n t)").bitcast(I32))
             table.append(words)
-        w2_raw = [load_w("w2", w2, g) for g in range(PASSES)]
-        w1_raw = [load_w("w1", w1, g) for g in range(PASSES)]
-        sig_sb = sb("sig_sb", [P, BLOCKS, S])
-        nc.sync.dma_start(out=sig_sb[:], in_=sig.rearrange("(b p) j -> p b j", p=P))
 
         ident = sb("ident", [P, P])
         make_identity(nc, ident[:])
 
         te_q = sb("te_q", [P, D])
         te_h = sb("te_h", [P, D])
-        nc.scalar.activation(te_q[:], te_col[:], ACT.Copy, scale=-1.0 / D)
-        nc.scalar.activation(te_h[:], te_col[:], ACT.Copy, scale=-2.0 / D)
+        nc.vector.tensor_scalar(te_q[:], te_col[:], -1.0 / D, None, ALU.mult)
+        nc.vector.tensor_scalar(te_h[:], te_col[:], -2.0 / D, None, ALU.mult)
+        warm = sb("warm", [P, 8])
+        nc.scalar.activation(warm[:, 2:3], te_q[:, 0:1], ACT.Sigmoid)
 
         def quantise(name, raw, b, grouped, on_scalar):
             dst = grouped.rearrange("p (c i t) -> p c t i", i=4, t=PACK)
@@ -83,11 +82,15 @@ def tile_picked_rate_p_kernel(tc, x_words, x_scales, w1, w2, te, sig, offs, out)
             nc.vector.quantize_mx(out=codes[:].bitcast(FP8X4), scales=scales[:], in_=grouped)
             return codes, scales
 
+        w2_bf = sb("w2_bf", [P, PASSES * BLOCKS, K_PASS], BF16)
+        w2_q = [[quantise("w2_%d%d" % (g, b), w2_raw[g], b, w2_bf[:, g * BLOCKS + b, :], True) for b in range(BLOCKS)] for g in range(PASSES)]
         picked_scales = sb("picked_scales", [P, S], U8)
         picked = [sb("picked%d" % g, [P, S], U32) for g in range(PASSES)]
-        nc.vector.tensor_copy(picked[0][:], table[0][:].indirect(offsets[:]))
         nc.vector.tensor_copy(picked_scales[:], scale_rows[:].indirect(offsets[:]))
+        nc.vector.tensor_copy(picked[0][:], table[0][:].indirect(offsets[:]))
         nc.vector.tensor_copy(picked[1][:], table[1][:].indirect(offsets[:]))
+
+        w1_raw = [load_w("w1", w1, g, "w_raw%d" % g) for g in range(PASSES)]
 
         def product(y, w_q, g):
             for b in range(BLOCKS):
@@ -104,25 +107,24 @@ def tile_picked_rate_p_kernel(tc, x_words, x_scales, w1, w2, te, sig, offs, out)
 
         yr = [bank("y%d" % b, [P, S]) for b in range(BLOCKS)]
         ya = [bank("y%d" % (BLOCKS + b), [P, S]) for b in range(BLOCKS)]
-        w2_bf = sb("w2_bf", [P, PASSES * BLOCKS, K_PASS], BF16, tag="scale_rows")
         for g in range(PASSES):
-            product(yr, [quantise("w2_%d%d" % (g, b), w2_raw[g], b, w2_bf[:, g * BLOCKS + b, :], b == 1) for b in range(BLOCKS)], g)
-        w1_bf = sb("w1_bf", [P, PASSES * BLOCKS, K_PASS], BF16, tag="scale_rows")
+            product(yr, w2_q[g], g)
+        sig_sb = sb("sig_sb", [P, BLOCKS, S], tag="table0")
+        nc.sync.dma_start(out=sig_sb[:], in_=sig.rearrange("(b p) j -> p b j", p=P))
+        w1_bf = sb("w1_bf", [P, PASSES * BLOCKS, K_PASS], BF16)
         for g in range(PASSES):
-            product(ya, [quantise("w1_%d%d" % (g, b), w1_raw[g], b, w1_bf[:, g * BLOCKS + b, :], False) for b in range(BLOCKS)], g)
+            product(ya, [quantise("w1_%d%d" % (g, b), w1_raw[g], b, w1_bf[:, g * BLOCKS + b, :], g == 0 and b == 0) for b in range(BLOCKS)], g)
 
         prod = sb("prod", [P, 2 * N])
 
         def log_argument(name, y, prod_out):
             small = sb(name + "_small", [P, D, N])
             for b in range(BLOCKS):
-                mag = sb("%s_mag%d" % (name, b), [P, D, V])
+                mag = sb("%s_mag%d" % (name, b), [P, D, V], tag="w_raw0" if (name, b) == ("r", 0) else None)
                 nc.scalar.activation(mag[:], y[b][:].rearrange("p (v d) -> p d v", d=D), ACT.Abs)
-                nc.scalar.activation(small[:, :, b * P : (b + 1) * P], mag[:], ACT.Exp, scale=-1.0)
-            half = sb(name + "_half", [P, 2, N])
-            nc.vector.tensor_scalar(half[:], small[:, 0:2, :], 1.0, None, ALU.add)
+                nc.scalar.activation(small[:, :, b * P : (b + 1) * P], mag[:], ACT.Sigmoid)
             pair = sb(name + "_pair", [P, 2, N])
-            nc.vector.scalar_tensor_tensor(pair[:], small[:, 2:4, :], 1.0, half[:], ALU.add, ALU.mult)
+            nc.vector.tensor_tensor(pair[:], small[:, 0:2, :], small[:, 2:4, :], ALU.mult)
             nc.vector.tensor_tensor(prod_out, pair[:, 0, :], pair[:, 1, :], ALU.mult)
 
         def relu_sum(name, y, shift):
@@ -140,6 +142,7 @@ def tile_picked_rate_p_kernel(tc, x_words, x_scales, w1, w2, te, sig, offs, out)
         log_argument("r", yr, prod[:, :N])
         log_argument("a", ya, prod[:, N:])
         relu_r = relu_sum("r", yr, 0.0)
+        relu_a = relu_sum("a", ya, 0.3 * D)
 
         sig_t = [bank("y%d" % h, [P, 2, N]) for h in range(D // 2)]
         for d in range(D):
@@ -149,17 +152,15 @@ def tile_picked_rate_p_kernel(tc, x_words, x_scales, w1, w2, te, sig, offs, out)
         logs = sb("logs", [P, 2 * N], tag="a_mag1")
         nc.scalar.activation(logs[:, :N], prod[:, :N], ACT.Ln)
         nc.scalar.activation(logs[:, N:], prod[:, N:], ACT.Ln)
-        warm = sb("warm", [P, 8])
         nc.scalar.activation(warm[:, 0:1], logs[:, N : N + 1], ACT.Exp)
         rel4 = sb("rel4", [P, N])
-        nc.vector.tensor_tensor(rel4[:], logs[:, :N], relu_r[:], ALU.add)
+        nc.vector.tensor_tensor(rel4[:], relu_r[:], logs[:, :N], ALU.subtract)
         rel4_t = bank("rel4_t", [P, N])
         for b in range(BLOCKS):
             cols = slice(b * P, (b + 1) * P)
             nc.tensor.transpose(rel4_t[:, cols], rel4[:, cols], ident[:])
-        relu_a = relu_sum("a", ya, 0.3 * D)
         amp4 = sb("amp4", [P, N])
-        nc.vector.tensor_tensor(amp4[:], logs[:, N:], relu_a[:], ALU.add)
+        nc.vector.tensor_tensor(amp4[:], relu_a[:], logs[:, N:], ALU.subtract)
 
         dec = [sb("dec%d" % d, [P, N]) for d in range(D)]
         dec_sq = [sb("dec_sq%d" % d, [P, N]) for d in range(D)]
@@ -170,49 +171,54 @@ def tile_picked_rate_p_kernel(tc, x_words, x_scales, w1, w2, te, sig, offs, out)
         for d in range(D):
             nc.scalar.activation(dec[d][:], rel4_t[:], ACT.Exp, scale=te_q[:, d : d + 1])
         for d in range(D):
-            nc.scalar.activation(tdec_sq[d][:], dec[d][:], ACT.Square, scale=te_col[:, d : d + 1])
+            nc.scalar.activation(tdec_sq[d][:], dec[d][:], ACT.Square, scale=te_q[:, d : d + 1])
 
         def weighted_sum(name, terms):
             acc = sb(name, [P, N])
-            nc.vector.tensor_scalar(acc[:], terms[0][:], te_col[:, 0:1], None, ALU.mult)
+            nc.vector.tensor_scalar(acc[:], terms[0][:], te_q[:, 0:1], None, ALU.mult)
             for d in range(1, D):
-                nc.vector.scalar_tensor_tensor(acc[:], terms[d][:], te_col[:, d : d + 1], acc[:], ALU.mult, ALU.add)
+                nc.vector.scalar_tensor_tensor(acc[:], terms[d][:], te_q[:, d : d + 1], acc[:], ALU.mult, ALU.add)
             return acc
 
         halves = [slice(b * P, (b + 1) * P) for b in range(BLOCKS)]
 
-        def turned_sum(totals, terms):
-            for i, term in enumerate(terms):
-                for total, cols in zip(totals, halves):
-                    nc.tensor.matmul(total, term[:, cols], ident[:], start=(i == 0), stop=(i == len(terms) - 1), is_transpose=True)
+        def add_turned(total, term, i, count):
+            nc.tensor.matmul(total, term, ident[:], start=(i == 0), stop=(i == count - 1), is_transpose=True)
 
-        s01 = [bank("s01_%d" % b, [P, 2, V]) for b in range(BLOCKS)]
-        s0 = [x[:, 0, :] for x in s01]
-        s1 = [x[:, 1, :] for x in s01]
-        turned_sum(s0, dec_sq)
-        turned_sum(s1, [weighted_sum("s1_v", dec_sq)])
-        har4 = sb("har4", [P, N])
-        for b, cols in enumerate(halves):
-            nc.vector.tensor_tensor(har4[:, cols], s1[b], amp4[:, cols], ALU.mult)
+        def turned_sum(tag, terms):
+            total = bank(tag, [P, N])
+            for cols in halves:
+                for i, term in enumerate(terms):
+                    add_turned(total[:, cols], term[:, cols], i, len(terms))
+            return total
+
+        def tt(name, a, b, op):
+            res = sb(name, [P, N])
+            nc.vector.tensor_tensor(res[:], a[:], b[:], op)
+            return res
+
+        def stt(name, a, c, b, op0, op1):
+            res = sb(name, [P, N])
+            nc.vector.scalar_tensor_tensor(res[:], a[:], c, b[:], op0, op1)
+            return res
+
+        s0 = turned_sum("s0", dec_sq)
+        s1 = turned_sum("s1", [weighted_sum("s1_v", dec_sq)])
+        har = tt("har", s1, amp4, ALU.mult)
         har_sq = sb("har_sq", [P, N])
-        nc.scalar.activation(har_sq[:], har4[:], ACT.Square, scale=1.0 / D)
+        nc.scalar.activation(har_sq[:], har[:], ACT.Square)
         nc.scalar.activation(warm[:, 1:2], har_sq[:, 0:1], ACT.Abs_reciprocal_sqrt)
         for d in range(D):
             nc.vector.tensor_tensor(dec_sig[d][:], sig_t[d // 2][:, d % 2, :], dec[d][:], ALU.mult)
-        t0 = [bank("y%d" % (BLOCKS + b), [P, V])[:] for b in range(BLOCKS)]
-        turned_sum(t0, dec_sig)
+        t0 = turned_sum("y2", dec_sig)
         s2 = [bank("s2", [P, V])[:], bank("rel4_t", [P, V])[:]]
-        turned_sum(s2, tdec_sq)
-        t1 = [bank("y%d" % b, [P, V])[:] for b in range(BLOCKS)]
-        turned_sum(t1, [weighted_sum("t1_v", dec_sig)])
-        amp_haa4 = sb("amp_haa4", [P, N])
-        for b, cols in enumerate(halves):
-            nc.vector.scalar_tensor_tensor(amp_haa4[:, cols], s0[b], 0.1, amp4[:, cols], ALU.add, ALU.mult)
-        c1 = sb("c1", [P, N])
-        nc.vector.scalar_tensor_tensor(c1[:], amp_haa4[:], 1.0 / (D * D), amp4[:], ALU.mult, ALU.mult)
-        c0 = sb("c0", [P, N])
-        for b, cols in enumerate(halves):
-            nc.vector.scalar_tensor_tensor(c0[:, cols], s0[b], 0.3, har_sq[:, cols], ALU.mult, ALU.subtract)
+        for d in range(D):
+            for total, cols in zip(s2, halves):
+                add_turned(total, tdec_sq[d][:, cols], d, D)
+        t1 = turned_sum("y3", [weighted_sum("t1_v", dec_sig)])
+        amp_haa4 = stt("amp_haa4", s0, 0.1, amp4, ALU.add, ALU.mult)
+        c1 = tt("c1", amp_haa4, amp4, ALU.mult)
+        c0 = stt("c0", s0, 0.3, har_sq, ALU.mult, ALU.subtract)
         e = sb("e", [P, N])
         det = sb("det", [P, N])
         root = sb("root", [P, N])
@@ -224,21 +230,13 @@ def tile_picked_rate_p_kernel(tc, x_words, x_scales, w1, w2, te, sig, offs, out)
         for cols in halves:
             nc.scalar.activation(root[:, cols], det[:, cols], ACT.Abs_reciprocal_sqrt)
         for cols in halves:
-            nc.scalar.activation(inv[:, cols], root[:, cols], ACT.Square, scale=0.5)
-        t0p = sb("t0p", [P, N])
-        for b, cols in enumerate(halves):
-            nc.vector.scalar_tensor_tensor(t0p[:, cols], amp4[:, cols], 0.1 / D, t0[b], ALU.mult, ALU.add)
-        n1 = sb("n1", [P, N])
-        n2 = sb("n2", [P, N])
-        num = sb("num", [P, N])
+            nc.scalar.activation(inv[:, cols], root[:, cols], ACT.Square)
+        t0p = stt("t0p", amp4, 0.1 / D, t0, ALU.mult, ALU.add)
+        n2 = tt("n2", t1, amp_haa4, ALU.mult)
+        n1 = tt("n1", t0p, har, ALU.mult)
+        num = tt("num", n2, n1, ALU.subtract)
         step = sb("step", [P, N])
         res = sb("res", [P, N])
-        for b, cols in enumerate(halves):
-            nc.vector.tensor_tensor(n2[:, cols], t1[b], amp_haa4[:, cols], ALU.mult)
-        for cols in halves:
-            nc.vector.tensor_tensor(n1[:, cols], t0p[:, cols], har4[:, cols], ALU.mult)
-        for cols in halves:
-            nc.vector.tensor_tensor(num[:, cols], n1[:, cols], n2[:, cols], ALU.subtract)
         for cols in halves:
             nc.vector.tensor_tensor(step[:, cols], num[:, cols], inv[:, cols], ALU.mult)
         for cols in halves:

from contextlib import ExitStack

import concourse.mybir as mybir
from concourse.masks import make_identity

K, T, S, D, N = 1024, 2048, 512, 4, 256
V = S // D
P = 128
PACK = 4
K_PASS = P * PACK
PASSES = K // K_PASS
BLOCKS = N // P
FLOPS = 2 * 2 * K * S * N
BYTES = K * T + K * T // 32 + 2 * K * N * 4 + S * 4 + N * S * 4 + P * (S // 16) * 2 + N * V * 4

F32 = mybir.dt.float32
BF16 = mybir.dt.bfloat16
I32 = mybir.dt.int32
U32 = mybir.dt.uint32
U16 = mybir.dt.uint16
U8 = mybir.dt.uint8
FP8X4 = mybir.dt.float8_e4m3fn_x4
ALU = mybir.AluOpType
ACT = mybir.ActivationFunctionType


def tile_picked_rate_p_kernel(tc, x_words, x_scales, w1, w2, te, sig, offs, out):
    nc = tc.nc
    with ExitStack() as ctx:
        keep = ctx.enter_context(tc.tile_pool(name="keep", bufs=1))
        psum = ctx.enter_context(tc.psum_pool(name="psum", bufs=1))

        def sb(name, shape, dtype=F32, tag=None):
            return keep.tile(shape, dtype, name=name, tag=tag or name, align_bytes=64)

        def bank(tag, shape):
            return psum.tile(shape, F32, name=tag, tag=tag)

        offsets = keep.tile([P, S // 16], U16, name="offsets")
        nc.sync.dma_start(offsets[:], offs)
        te_col = sb("te_col", [P, D])
        nc.sync.dma_start(out=te_col[:], in_=te[0:1, :].rearrange("o (v d) -> v (o d)", d=D))
        scale_rows = sb("scale_rows", [P, T], U8)
        nc.gpsimd.memset(scale_rows[:].bitcast(I32), 0)
        for quad in range(4):
            nc.scalar.dma_start(
                out=scale_rows[32 * quad : 32 * quad + 4 * PASSES, :].bitcast(I32),
                in_=x_scales[:, 4 * quad : 4 * quad + 4, :].bitcast(I32),
            )

        def load_w(name, w, g, tag=None):
            raw = sb("%s_raw%d" % (name, g), [P, PACK, N], tag=tag)
            nc.sync.dma_start(out=raw[:], in_=w[g * K_PASS : (g + 1) * K_PASS, :].rearrange("(p j) m -> p j m", j=PACK))
            return raw

        w2_raw = [load_w("w2", w2, g, "w_raw%d" % g) for g in range(PASSES)]
        table = []
        for g in range(PASSES):
            words = sb("table%d" % g, [P, T], U32)
            nc.sync.dma_start(out=words[:].bitcast(I32), in_=x_words[g].rearrange("p n t -> p (n t)").bitcast(I32))
            table.append(words)

        ident = sb("ident", [P, P])
        make_identity(nc, ident[:])

        te_q = sb("te_q", [P, D])
        te_h = sb("te_h", [P, D])
        nc.vector.tensor_scalar(te_q[:], te_col[:], -1.0 / D, None, ALU.mult)
        nc.vector.tensor_scalar(te_h[:], te_col[:], -2.0 / D, None, ALU.mult)
        warm = sb("warm", [P, 8])
        nc.scalar.activation(warm[:, 2:3], te_q[:, 0:1], ACT.Sigmoid)

        def quantise(name, raw, b, grouped, on_scalar):
            dst = grouped.rearrange("p (c i t) -> p c t i", i=4, t=PACK)
            src = raw[:, :, b * P : (b + 1) * P].rearrange("p t (c i) -> p c t i", i=4)
            if on_scalar:
                nc.scalar.copy(dst, src)
            else:
                nc.vector.tensor_copy(dst, src)
            codes = sb(name + "_codes", [P, P], U32)
            scales = sb(name + "_scales", [P, P], U8)
            nc.vector.quantize_mx(out=codes[:].bitcast(FP8X4), scales=scales[:], in_=grouped)
            return codes, scales

        w2_bf = sb("w2_bf", [P, PASSES * BLOCKS, K_PASS], BF16)
        w2_q = [[quantise("w2_%d%d" % (g, b), w2_raw[g], b, w2_bf[:, g * BLOCKS + b, :], True) for b in range(BLOCKS)] for g in range(PASSES)]
        picked_scales = sb("picked_scales", [P, S], U8)
        picked = [sb("picked%d" % g, [P, S], U32) for g in range(PASSES)]
        nc.vector.tensor_copy(picked_scales[:], scale_rows[:].indirect(offsets[:]))
        nc.vector.tensor_copy(picked[0][:], table[0][:].indirect(offsets[:]))
        nc.vector.tensor_copy(picked[1][:], table[1][:].indirect(offsets[:]))

        w1_raw = [load_w("w1", w1, g, "w_raw%d" % g) for g in range(PASSES)]

        def product(y, w_q, g):
            for b in range(BLOCKS):
                codes, scales = w_q[b]
                nc.tensor.matmul_mx(
                    out=y[b][:],
                    lhsT=codes[:].bitcast(FP8X4),
                    lhsT_scale=scales[:],
                    rhs=picked[g][:].bitcast(FP8X4),
                    rhs_scale=picked_scales[4 * g :, :],
                    start=(g == 0),
                    stop=(g == PASSES - 1),
                )

        yr = [bank("y%d" % b, [P, S]) for b in range(BLOCKS)]
        ya = [bank("y%d" % (BLOCKS + b), [P, S]) for b in range(BLOCKS)]
        for g in range(PASSES):
            product(yr, w2_q[g], g)
        sig_sb = sb("sig_sb", [P, BLOCKS, S], tag="table0")
        nc.sync.dma_start(out=sig_sb[:], in_=sig.rearrange("(b p) j -> p b j", p=P))
        w1_bf = sb("w1_bf", [P, PASSES * BLOCKS, K_PASS], BF16)
        for g in range(PASSES):
            product(ya, [quantise("w1_%d%d" % (g, b), w1_raw[g], b, w1_bf[:, g * BLOCKS + b, :], g == 0 and b == 0) for b in range(BLOCKS)], g)

        prod = sb("prod", [P, 2 * N])

        def log_argument(name, y, prod_out):
            small = sb(name + "_small", [P, D, N])
            for b in range(BLOCKS):
                mag = sb("%s_mag%d" % (name, b), [P, D, V], tag="w_raw0" if (name, b) == ("r", 0) else None)
                nc.scalar.activation(mag[:], y[b][:].rearrange("p (v d) -> p d v", d=D), ACT.Abs)
                nc.scalar.activation(small[:, :, b * P : (b + 1) * P], mag[:], ACT.Sigmoid)
            pair = sb(name + "_pair", [P, 2, N])
            nc.vector.tensor_tensor(pair[:], small[:, 0:2, :], small[:, 2:4, :], ALU.mult)
            nc.vector.tensor_tensor(prod_out, pair[:, 0, :], pair[:, 1, :], ALU.mult)

        def relu_sum(name, y, shift):
            relu = sb(name + "_relu", [P, N])
            for d in range(D):
                for b in range(BLOCKS):
                    cols = slice(b * P, (b + 1) * P)
                    y_d = y[b][:, d::D]
                    if d == 0:
                        nc.vector.tensor_scalar(relu[:, cols], y_d, 0.0, shift, ALU.max, ALU.add)
                    else:
                        nc.vector.scalar_tensor_tensor(relu[:, cols], y_d, 0.0, relu[:, cols], ALU.max, ALU.add)
            return relu

        log_argument("r", yr, prod[:, :N])
        log_argument("a", ya, prod[:, N:])
        relu_r = relu_sum("r", yr, 0.0)
        relu_a = relu_sum("a", ya, 0.3 * D)

        sig_t = [bank("y%d" % h, [P, 2, N]) for h in range(D // 2)]
        for d in range(D):
            for b in range(BLOCKS):
                nc.tensor.transpose(sig_t[d // 2][:, d % 2, b * P : (b + 1) * P], sig_sb[:, b, d::D], ident[:])

        logs = sb("logs", [P, 2 * N], tag="a_mag1")
        nc.scalar.activation(logs[:, :N], prod[:, :N], ACT.Ln)
        nc.scalar.activation(logs[:, N:], prod[:, N:], ACT.Ln)
        nc.scalar.activation(warm[:, 0:1], logs[:, N : N + 1], ACT.Exp)
        rel4 = sb("rel4", [P, N])
        nc.vector.tensor_tensor(rel4[:], relu_r[:], logs[:, :N], ALU.subtract)
        rel4_t = bank("rel4_t", [P, N])
        for b in range(BLOCKS):
            cols = slice(b * P, (b + 1) * P)
            nc.tensor.transpose(rel4_t[:, cols], rel4[:, cols], ident[:])
        amp4 = sb("amp4", [P, N])
        nc.vector.tensor_tensor(amp4[:], relu_a[:], logs[:, N:], ALU.subtract)

        dec = [sb("dec%d" % d, [P, N]) for d in range(D)]
        dec_sq = [sb("dec_sq%d" % d, [P, N]) for d in range(D)]
        tdec_sq = [sb("tdec_sq%d" % d, [P, N]) for d in range(D)]
        dec_sig = [sb("dec_sig%d" % d, [P, N]) for d in range(D)]
        for d in range(D):
            nc.scalar.activation(dec_sq[d][:], rel4_t[:], ACT.Exp, scale=te_h[:, d : d + 1])
        for d in range(D):
            nc.scalar.activation(dec[d][:], rel4_t[:], ACT.Exp, scale=te_q[:, d : d + 1])
        for d in range(D):
            nc.scalar.activation(tdec_sq[d][:], dec[d][:], ACT.Square, scale=te_q[:, d : d + 1])

        def weighted_sum(name, terms):
            acc = sb(name, [P, N])
            nc.vector.tensor_scalar(acc[:], terms[0][:], te_q[:, 0:1], None, ALU.mult)
            for d in range(1, D):
                nc.vector.scalar_tensor_tensor(acc[:], terms[d][:], te_q[:, d : d + 1], acc[:], ALU.mult, ALU.add)
            return acc

        halves = [slice(b * P, (b + 1) * P) for b in range(BLOCKS)]

        def add_turned(total, term, i, count):
            nc.tensor.matmul(total, term, ident[:], start=(i == 0), stop=(i == count - 1), is_transpose=True)

        def turned_sum(tag, terms):
            total = bank(tag, [P, N])
            for cols in halves:
                for i, term in enumerate(terms):
                    add_turned(total[:, cols], term[:, cols], i, len(terms))
            return total

        def tt(name, a, b, op):
            res = sb(name, [P, N])
            nc.vector.tensor_tensor(res[:], a[:], b[:], op)
            return res

        def stt(name, a, c, b, op0, op1):
            res = sb(name, [P, N])
            nc.vector.scalar_tensor_tensor(res[:], a[:], c, b[:], op0, op1)
            return res

        s0 = turned_sum("s0", dec_sq)
        s1 = turned_sum("s1", [weighted_sum("s1_v", dec_sq)])
        har = tt("har", s1, amp4, ALU.mult)
        har_sq = sb("har_sq", [P, N])
        nc.scalar.activation(har_sq[:], har[:], ACT.Square)
        nc.scalar.activation(warm[:, 1:2], har_sq[:, 0:1], ACT.Abs_reciprocal_sqrt)
        for d in range(D):
            nc.vector.tensor_tensor(dec_sig[d][:], sig_t[d // 2][:, d % 2, :], dec[d][:], ALU.mult)
        t0 = turned_sum("y2", dec_sig)
        s2 = [bank("s2", [P, V])[:], bank("rel4_t", [P, V])[:]]
        for d in range(D):
            for total, cols in zip(s2, halves):
                add_turned(total, tdec_sq[d][:, cols], d, D)
        t1 = turned_sum("y3", [weighted_sum("t1_v", dec_sig)])
        amp_haa4 = stt("amp_haa4", s0, 0.1, amp4, ALU.add, ALU.mult)
        c1 = tt("c1", amp_haa4, amp4, ALU.mult)
        c0 = stt("c0", s0, 0.3, har_sq, ALU.mult, ALU.subtract)
        e = sb("e", [P, N])
        det = sb("det", [P, N])
        root = sb("root", [P, N])
        inv = sb("inv", [P, N])
        for b, cols in enumerate(halves):
            nc.vector.tensor_tensor(e[:, cols], s2[b], c1[:, cols], ALU.mult)
        for cols in halves:
            nc.vector.scalar_tensor_tensor(det[:, cols], c0[:, cols], 0.03, e[:, cols], ALU.add, ALU.add)
        for cols in halves:
            nc.scalar.activation(root[:, cols], det[:, cols], ACT.Abs_reciprocal_sqrt)
        for cols in halves:
            nc.scalar.activation(inv[:, cols], root[:, cols], ACT.Square)
        t0p = stt("t0p", amp4, 0.1 / D, t0, ALU.mult, ALU.add)
        n2 = tt("n2", t1, amp_haa4, ALU.mult)
        n1 = tt("n1", t0p, har, ALU.mult)
        num = tt("num", n2, n1, ALU.subtract)
        step = sb("step", [P, N])
        res = sb("res", [P, N])
        for cols in halves:
            nc.vector.tensor_tensor(step[:, cols], num[:, cols], inv[:, cols], ALU.mult)
        for cols in halves:
            nc.vector.scalar_tensor_tensor(res[:, cols], rel4[:, cols], 1.0 / D, step[:, cols], ALU.mult, ALU.add)
            nc.sync.dma_start(out=out[cols, :], in_=res[:, cols])
